import numpy as np
import ml_dtypes


def mxq(x, axis, fmt="e4m3"):
    dtype, down = {"e4m3": (ml_dtypes.float8_e4m3fn, 7), "e5m2": (ml_dtypes.float8_e5m2, 14)}[fmt]
    v = np.moveaxis(np.asarray(x, np.float32).astype(ml_dtypes.bfloat16).astype(np.float64), axis, -1)
    blocks = v.reshape(v.shape[:-1] + (-1, 32))
    amax = np.abs(blocks).max(-1, keepdims=True)
    byte = np.maximum(np.where(amax > 0, np.frexp(amax)[1] - 1 + 127, 0) - down, 1)
    scale = np.exp2(byte - 127.0)
    codes = (blocks / scale).astype(np.float32).astype(dtype).astype(np.float64)
    return np.moveaxis((codes * scale).reshape(v.shape), -1, axis)


WIDE = False


def mx_kscale(k):
    if not WIDE:
        return np.ones(k)
    levels = np.array([10, -10, 5, -5, 0])
    if k % 512:
        return np.exp2(np.random.permutation(np.resize(levels, k // 32))).repeat(32)
    a = np.empty((k // 512, 16))
    for p in range(k // 512):
        a[p, :8] = np.random.permutation(np.resize(levels, 8))
        for g in range(8):
            far = levels[np.abs(levels - a[p, g]) >= 10]
            a[p, g + 8] = far[np.random.randint(len(far))]
    return np.exp2(a.ravel()).repeat(32)


def f64(x):
    return np.asarray(x).astype(np.float64)


def striped(idx):
    return np.tile(np.asarray(idx).reshape(-1, 16).T, (8, 1)).astype(np.uint16)


def unstriped(offs):
    return offs[:16].T.reshape(-1).astype(np.int64)


def striped8(idx):
    return np.asarray(idx).reshape(8, -1, 16).transpose(0, 2, 1).reshape(128, -1).astype(np.uint16)


def unstriped8(offs):
    return offs.reshape(8, 16, -1).transpose(0, 2, 1).reshape(8, -1).astype(np.int64)


def pick8(x, idx, run):
    r = np.arange(len(x))
    return x[r[:, None], idx[r % (8 * run) // run]]


E2M1 = np.array([0.0, 0.5, 1.0, 1.5, 2.0, 3.0, 4.0, 6.0, -0.0, -0.5, -1.0, -1.5, -2.0, -3.0, -4.0, -6.0])


def pack_weight(w, fmt):
    k, n = w.shape
    w = f64(np.asarray(w, np.float32).astype(ml_dtypes.bfloat16)).reshape(k // 32, 32, n)
    amax = np.abs(w).max(1)
    if fmt == "e4m3":
        byte = np.frexp(amax)[1] - 1 + 127 - 7
    else:
        mant, ex = np.frexp(amax / 6.0)
        byte = np.where(mant > 0.5, ex, ex - 1) + 127
    byte = np.clip(np.where(amax > 0, byte, 1), 1, 254)
    scaled = (w * np.exp2(127.0 - byte)[:, None, :]).reshape(k, n).astype(np.float32)
    by_word = np.ascontiguousarray(scaled.reshape(k // 512, 128, 4, n).transpose(0, 1, 3, 2))
    if fmt == "e4m3":
        words = by_word.astype(ml_dtypes.float8_e4m3fn).view(np.uint8)
    else:
        c = by_word.astype(ml_dtypes.float4_e2m1fn).view(np.uint8) & 0xF
        words = (c[..., 0::2] | (c[..., 1::2] << 4)).reshape(k // 512, 128, 2 * n)
    return np.ascontiguousarray(words), np.ascontiguousarray(byte.astype(np.uint8).reshape(k // 512, 16, n))


def unpack_weight(words, scales, fmt):
    g, _, n = scales.shape
    words = np.ascontiguousarray(words).reshape(g, 128, n, -1)
    if fmt == "e4m3":
        vals = words.view(ml_dtypes.float8_e4m3fn).astype(np.float64)
    else:
        nib = np.empty((g, 128, n, 4), np.uint8)
        nib[..., 0::2] = words & 0xF
        nib[..., 1::2] = words >> 4
        vals = E2M1[nib]
    vals = vals * np.repeat(np.exp2(scales.astype(np.float64) - 127.0), 8, axis=1)[..., None]
    return vals.transpose(0, 1, 3, 2).reshape(g * 512, n)


def sgn(shape):
    return np.random.uniform(0.5, 2.0, shape) * np.where(np.random.standard_normal(shape) < 0, -1.0, 1.0)


K, J, R, T, U, O, D, N, S, Z, E, G = 512, 512, 512, 1024, 1024, 256, 1024, 256, 512, 1024, 128, 512


def setup_inputs():
    n = np.random.standard_normal
    idx = np.random.permutation(T)[:J]
    idx2 = np.stack([np.random.permutation(U)[:J] for _ in range(8)])
    idx3 = np.stack([np.random.permutation(J)[:O] for _ in range(8)])
    idx4 = np.stack([np.random.permutation(D)[:O] for _ in range(8)])
    idx5 = np.random.permutation(Z)[:O]
    idx6 = np.stack([np.random.permutation(O)[:E] for _ in range(8)])
    idx7 = np.stack([np.random.permutation(G)[:E] for _ in range(8)])
    fk = mx_kscale(K)
    fr = mx_kscale(R)
    fs = mx_kscale(S)
    wp = pack_weight(n((K, R)) * 1 / np.sqrt(K) / fk[:, None] * fr, "e4m3")
    wbp = pack_weight(n((R, N)) * 1 / np.sqrt(R) / fr[:, None], "e2m1")
    xrp = pack_weight(n((S, Z)) / fs[:, None], "e2m1")
    wsp = pack_weight(n((S, N)) * 1 / np.sqrt(S) * fs[:, None], "e4m3")
    return {
        "ta": (np.random.randint(-7, 8, (K, T)).astype(np.float64)).astype(np.float32),
        "tb": (np.random.randint(-7, 8, (K, U)).astype(np.float64)).astype(np.float32),
        "ga": ((np.random.randint(10, 25, (K, 1)) / 64.0) * fk[:, None]).astype(np.float32),
        "gb": ((np.random.randint(4, 13, (K, 1)) / 64.0) * fk[:, None]).astype(np.float32),
        "w_words": wp[0],
        "w_scales": wp[1],
        "tl": (np.random.randint(-7, 8, (R, D)).astype(np.float64)).astype(np.float32),
        "sa": (np.random.uniform(0.5, 1.6, (R, 1))).astype(np.float32),
        "sl": ((np.random.randint(6, 19, (R, 1)) / 64.0) * fr[:, None]).astype(np.float32),
        "wb_words": wbp[0],
        "wb_scales": wbp[1],
        "xr_words": xrp[0],
        "xr_scales": xrp[1],
        "ws_words": wsp[0],
        "ws_scales": wsp[1],
        "so": (sgn((N, 1))).astype(np.float32),
        "offs": striped(idx),
        "offs2": striped8(idx2),
        "offs3": striped8(idx3),
        "offs4": striped8(idx4),
        "offs5": striped(idx5),
        "offs6": striped8(idx6),
        "offs7": striped8(idx7),
    }


def reference(ta, tb, ga, gb, w_words, w_scales, tl, sa, sl, wb_words, wb_scales, xr_words, xr_scales, ws_words, ws_scales, so, offs, offs2, offs3, offs4, offs5, offs6, offs7):
    idx = unstriped(offs)
    idx2 = unstriped8(offs2)
    idx3 = unstriped8(offs3)
    idx4 = unstriped8(offs4)
    idx5 = unstriped(offs5)
    idx6 = unstriped8(offs6)
    idx7 = unstriped8(offs7)
    wu = unpack_weight(w_words, w_scales, "e4m3")
    wbu = unpack_weight(wb_words, wb_scales, "e2m1")
    xru = unpack_weight(xr_words, xr_scales, "e2m1")
    wsu = unpack_weight(ws_words, ws_scales, "e4m3")
    xc = f64(ta)[:, idx] * f64(ga) + pick8(f64(tb), idx2, 64) * f64(gb)
    xcq = mxq(xc, 0, "e4m3")
    a = wu.T @ xcq
    hid = np.maximum(pick8(a, idx3, 64) * f64(sa), pick8(f64(tl), idx4, 64) * f64(sl))
    hidq = mxq(hid, 0, "e4m3")
    xridx5g = xru[:, idx5]
    p = wbu.T @ hidq + wsu.T @ xridx5g
    m0 = pick8(p, idx6, 16) * f64(so)
    y = np.zeros((N, G))
    y[np.arange(N)[:, None], idx7[np.arange(N) % 128 // 16]] = m0
    return y

@@ -1,0 +1,270 @@
+from contextlib import ExitStack
+
+import concourse.mybir as mybir
+
+F32 = mybir.dt.float32
+BF16 = mybir.dt.bfloat16
+I32 = mybir.dt.int32
+U32 = mybir.dt.uint32
+U16 = mybir.dt.uint16
+U8 = mybir.dt.uint8
+FP8X4 = mybir.dt.float8_e4m3fn_x4
+FP4X4 = mybir.dt.float4_e2m1fn_x4
+ADD = mybir.AluOpType.add
+MAX = mybir.AluOpType.max
+COPY = mybir.ActivationFunctionType.Copy
+
+P = 128
+PACK = 4
+K, J, R, O, N, S, Z, E, G = 512, 512, 512, 256, 256, 512, 1024, 128, 512
+TABLE = 1024
+FLOPS = 2 * (K * R * J + R * N * O + S * N * O)
+
+
+def tile_picked_basedetail_plain_one_codedlevel_reminder_posted_kernel(
+    tc, ta, tb, ga, gb, w_words, w_scales, tl, sa, sl, wb_words, wb_scales, xr_words, xr_scales,
+    ws_words, ws_scales, so, offs, offs2, offs3, offs4, offs5, offs6, offs7, out,
+):
+    nc = tc.nc
+    with ExitStack() as ctx:
+        lists = ctx.enter_context(tc.tile_pool(name="lists", bufs=1))
+        keep = ctx.enter_context(tc.tile_pool(name="keep", bufs=1))
+        psum = ctx.enter_context(tc.psum_pool(name="psum", bufs=1))
+
+        def sb(name, shape, dtype, tag=None):
+            return keep.tile(shape, dtype, name=name, tag=tag or name, align_bytes=64)
+
+        def load_list(name, src):
+            tile = lists.tile(list(src.shape), U16, name=name)
+            nc.sync.dma_start(tile[:], src)
+            return tile
+
+        def load_plane(name, table, t):
+            tile = sb(name, [P, TABLE], F32)
+            nc.sync.dma_start(out=tile[:], in_=table.rearrange("(p t) u -> t p u", t=PACK)[t])
+            return tile
+
+        def load_steps(name, vec, queue):
+            tile = sb(name, [P, PACK], F32)
+            queue.dma_start(out=tile[:], in_=vec.rearrange("(p t) o -> p (t o)", t=PACK))
+            return tile
+
+        def stage_scales(name, scales, width):
+            staged = sb(name + "_staged", [P, 2, width], U8)
+            for u in range(2):
+                nc.sync.dma_start(
+                    out=staged[64 * u : 64 * u + 4].bitcast(I32),
+                    in_=scales[0, 8 * u : 8 * u + 8, :].rearrange("(q i) c -> i q c", i=4).bitcast(I32),
+                )
+            plane = sb(name, [P, width], U8)
+            nc.vector.memset(plane[:].bitcast(I32), 0)
+            for q in range(4):
+                u = q // 2
+                nc.vector.tensor_copy(
+                    out=plane[32 * q : 32 * q + 4, :].bitcast(I32),
+                    in_=staged[64 * u : 64 * u + 4, q % 2, :].bitcast(I32),
+                )
+            return plane
+
+        def load_scales(name, scales, width):
+            plane = sb(name, [P, width], U8)
+            nc.gpsimd.memset(plane[:].bitcast(I32), 0)
+            for q in range(4):
+                nc.gpsimd.dma_start(
+                    out=plane[32 * q : 32 * q + 4, :].bitcast(I32),
+                    in_=scales[0, 4 * q : 4 * q + 4, :].bitcast(I32),
+                )
+            return plane
+
+        def fetch(dst, window, offsets, scale):
+            nc.scalar.activation(out=dst, in_=window[:].indirect(offsets), func=COPY, scale=scale)
+
+        a_win, b_win, l_win = [], [], []
+        ga_sb = load_steps("ga_sb", ga, nc.scalar)
+        gb_sb = load_steps("gb_sb", gb, nc.scalar)
+
+        ws_plane = load_scales("ws_plane", ws_scales, N)
+        wb_plane = load_scales("wb_plane", wb_scales, N)
+        a_win.append(load_plane("ta0", ta, 0))
+        idx = load_list("idx", offs)
+        b_win.append(load_plane("tb0", tb, 0))
+        idx2 = load_list("idx2", offs2)
+        a_win.append(load_plane("ta1", ta, 1))
+        b_win.append(load_plane("tb1", tb, 1))
+        xr_win = sb("xr_win", [P, Z], U16)
+        nc.sync.dma_start(out=xr_win[:].bitcast(I32), in_=xr_words[0].bitcast(I32))
+        xr_plane = stage_scales("xr_plane", xr_scales, Z)
+        idx5 = load_list("idx5", offs5)
+        a_win.append(load_plane("ta2", ta, 2))
+        b_win.append(load_plane("tb2", tb, 2))
+        w_plane_raw = stage_scales("w_plane_raw", w_scales, R)
+        b_win.append(load_plane("tb3", tb, 3))
+        w_raw = sb("w_raw", [P, R], I32)
+        nc.sync.dma_start(out=w_raw[:], in_=w_words[0].rearrange("p c t -> p (c t)").bitcast(I32))
+        a_win.append(load_plane("ta3", ta, 3))
+        sl_sb = load_steps("sl_sb", sl, nc.sync)
+        idx4 = load_list("idx4", offs4)
+        l_win.append(load_plane("tl0", tl, 0))
+        l_win.append(load_plane("tl1", tl, 1))
+        l_win.append(load_plane("tl2", tl, 2))
+        l_win.append(load_plane("tl3", tl, 3))
+        sa_sb = load_steps("sa_sb", sa, nc.sync)
+        idx3 = load_list("idx3", offs3)
+        ws_codes = sb("ws_codes", [P, N], I32)
+        nc.sync.dma_start(out=ws_codes[:], in_=ws_words[0].rearrange("p c t -> p (c t)").bitcast(I32))
+        wb_codes = sb("wb_codes", [P, 2 * N], U8)
+        nc.sync.dma_start(out=wb_codes[:].bitcast(I32), in_=wb_words[0].bitcast(I32))
+        so_sb = sb("so_sb", [P, 2], F32)
+        with nc.allow_non_contiguous_dma(reason="one weight for each output feature, one to a partition"):
+            nc.sync.dma_start(out=so_sb[:], in_=so.rearrange("(t p) o -> p (t o)", p=P))
+        idx6 = load_list("idx6", offs6)
+        idx7 = load_list("idx7", offs7)
+
+        pages = [sb("page%d" % n, [P, G], F32) for n in range(2)]
+        for page in pages:
+            nc.vector.memset(page[:], 0.0)
+
+        JH = J // 2
+        JQ = J // 4
+        xa = [sb("xa%d" % u, [P, 2, J], F32) for u in range(2)]
+        xb = [sb("xb%d" % u, [P, 2, J], F32) for u in range(2)]
+        xc = [sb("xc%d" % h, [P, JH, PACK], BF16) for h in range(2)]
+
+        def add_pair(u, first, width):
+            cols = slice(first, first + width)
+            h, start = divmod(first, JH)
+            nc.vector.tensor_tensor(
+                out=xc[h][:, start : start + width, 2 * u : 2 * u + 2],
+                in0=xa[u][:, :, cols].rearrange("p t j -> p j t"),
+                in1=xb[u][:, :, cols].rearrange("p t j -> p j t"),
+                op=ADD,
+            )
+
+        for t in range(PACK):
+            if t < PACK - 1:
+                fetch(xa[t // 2][:, t % 2, :], a_win[t], idx[:], ga_sb[:, t : t + 1])
+            fetch(xb[t // 2][:, t % 2, :], b_win[t], idx2[:], gb_sb[:, t : t + 1])
+            if t == PACK - 1:
+                for first in range(0, J, JQ):
+                    fetch(xa[1][:, 1, first : first + JQ], a_win[t],
+                          idx[:, first // 16 : (first + JQ) // 16], ga_sb[:, t : t + 1])
+            if t == 1:
+                for h in range(2):
+                    add_pair(0, h * JH, JH)
+                xr_codes = sb("xr_codes", [P, O], U16)
+                nc.vector.tensor_copy(out=xr_codes[:], in_=xr_win[:].indirect(idx5[:]))
+                xr_sc = sb("xr_sc", [P, O], U8)
+                nc.vector.tensor_copy(out=xr_sc[:], in_=xr_plane[:].indirect(idx5[:]))
+            if t == 2:
+                w_codes = sb("w_codes", [P, PACK, P], I32)
+                nc.vector.tensor_copy(
+                    out=w_codes[:].rearrange("p t (c i) -> p c t i", i=4),
+                    in_=w_raw[:].rearrange("p (c i t) -> p c t i", i=4, t=PACK),
+                )
+                w_plane = sb("w_plane", [P, PACK, P], U8)
+                nc.vector.tensor_copy(out=w_plane[:], in_=w_plane_raw[:].rearrange("p (m t) -> p t m", t=PACK))
+
+        xc_codes = [sb("xc_codes%d" % h, [P, JH], U32) for h in range(2)]
+        xc_plane = [sb("xc_plane%d" % h, [P, JH], U8) for h in range(2)]
+        for first in range(0, J, JQ):
+            add_pair(1, first, JQ)
+        for h in range(2):
+            nc.vector.quantize_mx(out=xc_codes[h][:].bitcast(FP8X4), scales=xc_plane[h][:],
+                                  in_=xc[h][:].rearrange("p j t -> p (j t)"))
+
+        a0_acc = [psum.tile([P, JH], F32, name="a0_acc%d" % h) for h in range(2)]
+        a_acc = [None] + [psum.tile([P, J], F32, name="a_acc%d" % t) for t in range(1, PACK)]
+
+        def first_product(t, h):
+            nc.tensor.matmul_mx(
+                out=a0_acc[h][:] if t == 0 else a_acc[t][:, h * JH : (h + 1) * JH],
+                lhsT=w_codes[:, t, :].bitcast(FP8X4), lhsT_scale=w_plane[:, t, :],
+                rhs=xc_codes[h][:].bitcast(FP8X4), rhs_scale=xc_plane[h][:],
+                start=True, stop=True,
+            )
+
+        first_product(0, 0)
+        first_product(0, 1)
+        for t in range(1, PACK):
+            for h in range(2):
+                first_product(t, h)
+
+        OH = O // 2
+        ha = []
+        hl = [sb("hl%d" % u, [P, 2, O], F32) for u in range(2)]
+        hid = [sb("hid%d" % h, [P, OH, PACK], BF16) for h in range(2)]
+        a_sb = [sb("a_sb%d" % t, [P, J], F32) for t in range(PACK)]
+
+        def max_pair(u, h):
+            cols = slice(h * OH, (h + 1) * OH)
+            nc.vector.tensor_tensor(
+                out=hid[h][:, :, 2 * u : 2 * u + 2],
+                in0=ha[u][:, :, cols].rearrange("p t o -> p o t"),
+                in1=hl[u][:, :, cols].rearrange("p t o -> p o t"),
+                op=MAX,
+            )
+
+        def fetch_level(t):
+            fetch(hl[t // 2][:, t % 2, :], l_win[t], idx4[:], sl_sb[:, t : t + 1])
+
+        for t in range(PACK):
+            fetch_level(t)
+        for h in range(2):
+            nc.vector.tensor_copy(out=a_sb[0][:, h * JH : (h + 1) * JH], in_=a0_acc[h][:])
+        for t in range(1, PACK):
+            nc.vector.tensor_copy(out=a_sb[t][:], in_=a_acc[t][:])
+        ha.append(sb("ha0", [P, 2, O], F32, tag="tl3"))
+        for t in range(2):
+            fetch(ha[0][:, t, :], a_sb[t], idx3[:], sa_sb[:, t : t + 1])
+        ha.append(sb("ha1", [P, 2, O], F32))
+        fetch(ha[1][:, 0, :], a_sb[2], idx3[:], sa_sb[:, 2:3])
+        for h in range(2):
+            fetch(ha[1][:, 1, h * OH : (h + 1) * OH], a_sb[PACK - 1],
+                  idx3[:, h * OH // 16 : (h + 1) * OH // 16], sa_sb[:, PACK - 1 : PACK])
+        for u in range(2):
+            for h in range(2):
+                max_pair(u, h)
+        hid_codes = [sb("hid_codes%d" % h, [P, OH], U32) for h in range(2)]
+        hid_plane = [sb("hid_plane%d" % h, [P, OH], U8) for h in range(2)]
+        for h in range(2):
+            nc.vector.quantize_mx(out=hid_codes[h][:].bitcast(FP8X4), scales=hid_plane[h][:],
+                                  in_=hid[h][:].rearrange("p o t -> p (o t)"))
+
+        p0_acc = [psum.tile([P, OH], F32, name="p0_acc%d" % h) for h in range(2)]
+        p1_acc = psum.tile([P, O], F32, name="p1_acc")
+
+        def reminder_product(acc, n, cols):
+            nc.tensor.matmul_mx(
+                out=acc,
+                lhsT=ws_codes[:, n * P : (n + 1) * P].bitcast(FP8X4), lhsT_scale=ws_plane[:, n * P : (n + 1) * P],
+                rhs=xr_codes[:, cols].bitcast(FP4X4), rhs_scale=xr_sc[:, cols],
+                start=True, stop=False,
+            )
+
+        def output_product(acc, n, h, stop):
+            nc.tensor.matmul_mx(
+                out=acc,
+                lhsT=wb_codes[:, 2 * n * P : 2 * (n + 1) * P].bitcast(FP4X4),
+                lhsT_scale=wb_plane[:, n * P : (n + 1) * P],
+                rhs=hid_codes[h][:].bitcast(FP8X4), rhs_scale=hid_plane[h][:],
+                start=False, stop=stop,
+            )
+
+        for h in range(2):
+            reminder_product(p0_acc[h][:], 0, slice(h * OH, (h + 1) * OH))
+        reminder_product(p1_acc[:], 1, slice(0, O))
+        for h in range(2):
+            output_product(p0_acc[h][:], 0, h, True)
+        for h in range(2):
+            output_product(p1_acc[:, h * OH : (h + 1) * OH], 1, h, h == 1)
+
+        p_sb = [sb("p_sb%d" % n, [P, O], F32) for n in range(2)]
+        m0 = [sb("m0_%d" % n, [P, E], F32) for n in range(2)]
+        nc.scalar.copy(out=p_sb[0][:, 0:OH], in_=p0_acc[0][:])
+        nc.vector.tensor_copy(out=p_sb[0][:, OH:O], in_=p0_acc[1][:])
+        nc.vector.tensor_copy(out=p_sb[1][:], in_=p1_acc[:])
+        for n in range(2):
+            fetch(m0[n][:], p_sb[n], idx6[:], so_sb[:, n : n + 1])
+        for n in range(2):
+            nc.vector.tensor_copy(out=pages[n][:].indirect(idx7[:]), in_=m0[n][:])
+            nc.sync.dma_start(out=out[n * P : (n + 1) * P, :], in_=pages[n][:])

@@ -79,6 +79,9 @@ def tile_picked_basedetail_plain_one_codedlevel_reminder_posted_kernel(
         def fetch(dst, window, offsets, scale):
             nc.scalar.activation(out=dst, in_=window[:].indirect(offsets), func=COPY, scale=scale)
 
+        warm = sb("warm", [P, 2], F32)
+        nc.vector.memset(warm[:], 0.0)
+        nc.scalar.activation(out=warm[:, 1:2], in_=warm[:, 0:1], func=COPY)
         a_win, b_win, l_win = [], [], []
         ga_sb = load_steps("ga_sb", ga, nc.scalar)
         gb_sb = load_steps("gb_sb", gb, nc.scalar)

@@ -49,31 +49,12 @@ def tile_picked_basedetail_plain_one_codedlevel_reminder_posted_kernel(
             queue.dma_start(out=tile[:], in_=vec.rearrange("(p t) o -> p (t o)", t=PACK))
             return tile
 
-        def stage_scales(name, scales, width):
-            staged = sb(name + "_staged", [P, 2, width], U8)
-            for u in range(2):
-                nc.sync.dma_start(
-                    out=staged[64 * u : 64 * u + 4].bitcast(I32),
-                    in_=scales[0, 8 * u : 8 * u + 8, :].rearrange("(q i) c -> i q c", i=4).bitcast(I32),
-                )
+        def load_scales(name, scales, width, clear, queue):
             plane = sb(name, [P, width], U8)
-            nc.vector.memset(plane[:].bitcast(I32), 0)
-            for q in range(4):
-                u = q // 2
-                nc.vector.tensor_copy(
-                    out=plane[32 * q : 32 * q + 4, :].bitcast(I32),
-                    in_=staged[64 * u : 64 * u + 4, q % 2, :].bitcast(I32),
-                )
-            return plane
-
-        def load_scales(name, scales, width):
-            plane = sb(name, [P, width], U8)
-            nc.gpsimd.memset(plane[:].bitcast(I32), 0)
-            for q in range(4):
-                nc.gpsimd.dma_start(
-                    out=plane[32 * q : 32 * q + 4, :].bitcast(I32),
-                    in_=scales[0, 4 * q : 4 * q + 4, :].bitcast(I32),
-                )
+            clear.memset(plane[:].bitcast(I32), 0)
+            rows = scales[0].rearrange("(q i) c -> i q c", i=4)
+            for i in range(4):
+                queue.dma_start(out=plane[i:P:32, :].bitcast(I32), in_=rows[i].bitcast(I32))
             return plane
 
         def fetch(dst, window, offsets, scale):
@@ -86,21 +67,17 @@ def tile_picked_basedetail_plain_one_codedlevel_reminder_posted_kernel(
         ga_sb = load_steps("ga_sb", ga, nc.scalar)
         gb_sb = load_steps("gb_sb", gb, nc.scalar)
 
-        ws_plane = load_scales("ws_plane", ws_scales, N)
-        wb_plane = load_scales("wb_plane", wb_scales, N)
+        xr_plane = load_scales("xr_plane", xr_scales, Z, nc.gpsimd, nc.gpsimd)
         a_win.append(load_plane("ta0", ta, 0))
         idx = load_list("idx", offs)
         b_win.append(load_plane("tb0", tb, 0))
         idx2 = load_list("idx2", offs2)
         a_win.append(load_plane("ta1", ta, 1))
         b_win.append(load_plane("tb1", tb, 1))
-        xr_win = sb("xr_win", [P, Z], U16)
-        nc.sync.dma_start(out=xr_win[:].bitcast(I32), in_=xr_words[0].bitcast(I32))
-        xr_plane = stage_scales("xr_plane", xr_scales, Z)
         idx5 = load_list("idx5", offs5)
         a_win.append(load_plane("ta2", ta, 2))
         b_win.append(load_plane("tb2", tb, 2))
-        w_plane_raw = stage_scales("w_plane_raw", w_scales, R)
+        w_plane_raw = load_scales("w_plane_raw", w_scales, R, nc.vector, nc.sync)
         b_win.append(load_plane("tb3", tb, 3))
         w_raw = sb("w_raw", [P, R], I32)
         nc.sync.dma_start(out=w_raw[:], in_=w_words[0].rearrange("p c t -> p (c t)").bitcast(I32))
@@ -113,10 +90,14 @@ def tile_picked_basedetail_plain_one_codedlevel_reminder_posted_kernel(
         l_win.append(load_plane("tl3", tl, 3))
         sa_sb = load_steps("sa_sb", sa, nc.sync)
         idx3 = load_list("idx3", offs3)
+        xr_win = sb("xr_win", [P, Z], U16)
+        nc.sync.dma_start(out=xr_win[:].bitcast(I32), in_=xr_words[0].bitcast(I32))
         ws_codes = sb("ws_codes", [P, N], I32)
         nc.sync.dma_start(out=ws_codes[:], in_=ws_words[0].rearrange("p c t -> p (c t)").bitcast(I32))
         wb_codes = sb("wb_codes", [P, 2 * N], U8)
         nc.sync.dma_start(out=wb_codes[:].bitcast(I32), in_=wb_words[0].bitcast(I32))
+        ws_plane = load_scales("ws_plane", ws_scales, N, nc.vector, nc.sync)
+        wb_plane = load_scales("wb_plane", wb_scales, N, nc.vector, nc.sync)
         so_sb = sb("so_sb", [P, 2], F32)
         with nc.allow_non_contiguous_dma(reason="one weight for each output feature, one to a partition"):
             nc.sync.dma_start(out=so_sb[:], in_=so.rearrange("(t p) o -> p (t o)", p=P))
@@ -154,8 +135,6 @@ def tile_picked_basedetail_plain_one_codedlevel_reminder_posted_kernel(
             if t == 1:
                 for h in range(2):
                     add_pair(0, h * JH, JH)
-                xr_codes = sb("xr_codes", [P, O], U16)
-                nc.vector.tensor_copy(out=xr_codes[:], in_=xr_win[:].indirect(idx5[:]))
                 xr_sc = sb("xr_sc", [P, O], U8)
                 nc.vector.tensor_copy(out=xr_sc[:], in_=xr_plane[:].indirect(idx5[:]))
             if t == 2:
@@ -195,7 +174,6 @@ def tile_picked_basedetail_plain_one_codedlevel_reminder_posted_kernel(
         OH = O // 2
         ha = []
         hl = [sb("hl%d" % u, [P, 2, O], F32) for u in range(2)]
-        hid = [sb("hid%d" % h, [P, OH, PACK], BF16) for h in range(2)]
         a_sb = [sb("a_sb%d" % t, [P, J], F32) for t in range(PACK)]
 
         def max_pair(u, h):
@@ -216,6 +194,9 @@ def tile_picked_basedetail_plain_one_codedlevel_reminder_posted_kernel(
             nc.vector.tensor_copy(out=a_sb[0][:, h * JH : (h + 1) * JH], in_=a0_acc[h][:])
         for t in range(1, PACK):
             nc.vector.tensor_copy(out=a_sb[t][:], in_=a_acc[t][:])
+        xr_codes = sb("xr_codes", [P, O], U16)
+        nc.vector.tensor_copy(out=xr_codes[:], in_=xr_win[:].indirect(idx5[:]))
+        hid = [sb("hid0", [P, OH, PACK], BF16, tag="xr_win"), sb("hid1", [P, OH, PACK], BF16)]
         ha.append(sb("ha0", [P, 2, O], F32, tag="tl3"))
         for t in range(2):
             fetch(ha[0][:, t, :], a_sb[t], idx3[:], sa_sb[:, t : t + 1])

from contextlib import ExitStack

import concourse.mybir as mybir

F32 = mybir.dt.float32
BF16 = mybir.dt.bfloat16
I32 = mybir.dt.int32
U32 = mybir.dt.uint32
U16 = mybir.dt.uint16
U8 = mybir.dt.uint8
FP8X4 = mybir.dt.float8_e4m3fn_x4
FP4X4 = mybir.dt.float4_e2m1fn_x4
ADD = mybir.AluOpType.add
MAX = mybir.AluOpType.max
COPY = mybir.ActivationFunctionType.Copy

P = 128
PACK = 4
K, J, R, O, N, S, Z, E, G = 512, 512, 512, 256, 256, 512, 1024, 128, 512
TABLE = 1024
FLOPS = 2 * (K * R * J + R * N * O + S * N * O)


def tile_picked_basedetail_plain_one_codedlevel_reminder_posted_kernel(
    tc, ta, tb, ga, gb, w_words, w_scales, tl, sa, sl, wb_words, wb_scales, xr_words, xr_scales,
    ws_words, ws_scales, so, offs, offs2, offs3, offs4, offs5, offs6, offs7, out,
):
    nc = tc.nc
    with ExitStack() as ctx:
        lists = ctx.enter_context(tc.tile_pool(name="lists", bufs=1))
        keep = ctx.enter_context(tc.tile_pool(name="keep", bufs=1))
        psum = ctx.enter_context(tc.psum_pool(name="psum", bufs=1))

        def sb(name, shape, dtype, tag=None):
            return keep.tile(shape, dtype, name=name, tag=tag or name, align_bytes=64)

        def load_list(name, src):
            tile = lists.tile(list(src.shape), U16, name=name)
            nc.sync.dma_start(tile[:], src)
            return tile

        def load_plane(name, table, t):
            tile = sb(name, [P, TABLE], F32)
            nc.sync.dma_start(out=tile[:], in_=table.rearrange("(p t) u -> t p u", t=PACK)[t])
            return tile

        def load_steps(name, vec, queue):
            tile = sb(name, [P, PACK], F32)
            queue.dma_start(out=tile[:], in_=vec.rearrange("(p t) o -> p (t o)", t=PACK))
            return tile

        def load_scales(name, scales, width, clear, queue):
            plane = sb(name, [P, width], U8)
            clear.memset(plane[:].bitcast(I32), 0)
            rows = scales[0].rearrange("(q i) c -> i q c", i=4)
            for i in range(4):
                queue.dma_start(out=plane[i:P:32, :].bitcast(I32), in_=rows[i].bitcast(I32))
            return plane

        def fetch(dst, window, offsets, scale):
            nc.scalar.activation(out=dst, in_=window[:].indirect(offsets), func=COPY, scale=scale)

        warm = sb("warm", [P, 2], F32)
        nc.vector.memset(warm[:], 0.0)
        nc.scalar.activation(out=warm[:, 1:2], in_=warm[:, 0:1], func=COPY)
        a_win, b_win, l_win = [], [], []
        ga_sb = load_steps("ga_sb", ga, nc.scalar)
        gb_sb = load_steps("gb_sb", gb, nc.scalar)

        xr_plane = load_scales("xr_plane", xr_scales, Z, nc.gpsimd, nc.gpsimd)
        a_win.append(load_plane("ta0", ta, 0))
        idx = load_list("idx", offs)
        b_win.append(load_plane("tb0", tb, 0))
        idx2 = load_list("idx2", offs2)
        a_win.append(load_plane("ta1", ta, 1))
        b_win.append(load_plane("tb1", tb, 1))
        idx5 = load_list("idx5", offs5)
        a_win.append(load_plane("ta2", ta, 2))
        b_win.append(load_plane("tb2", tb, 2))
        w_plane_raw = load_scales("w_plane_raw", w_scales, R, nc.vector, nc.sync)
        b_win.append(load_plane("tb3", tb, 3))
        w_raw = sb("w_raw", [P, R], I32)
        nc.sync.dma_start(out=w_raw[:], in_=w_words[0].rearrange("p c t -> p (c t)").bitcast(I32))
        a_win.append(load_plane("ta3", ta, 3))
        sl_sb = load_steps("sl_sb", sl, nc.sync)
        idx4 = load_list("idx4", offs4)
        l_win.append(load_plane("tl0", tl, 0))
        l_win.append(load_plane("tl1", tl, 1))
        l_win.append(load_plane("tl2", tl, 2))
        l_win.append(load_plane("tl3", tl, 3))
        sa_sb = load_steps("sa_sb", sa, nc.sync)
        idx3 = load_list("idx3", offs3)
        xr_win = sb("xr_win", [P, Z], U16)
        nc.sync.dma_start(out=xr_win[:].bitcast(I32), in_=xr_words[0].bitcast(I32))
        ws_codes = sb("ws_codes", [P, N], I32)
        nc.sync.dma_start(out=ws_codes[:], in_=ws_words[0].rearrange("p c t -> p (c t)").bitcast(I32))
        wb_codes = sb("wb_codes", [P, 2 * N], U8)
        nc.sync.dma_start(out=wb_codes[:].bitcast(I32), in_=wb_words[0].bitcast(I32))
        ws_plane = load_scales("ws_plane", ws_scales, N, nc.vector, nc.sync)
        wb_plane = load_scales("wb_plane", wb_scales, N, nc.vector, nc.sync)
        so_sb = sb("so_sb", [P, 2], F32)
        with nc.allow_non_contiguous_dma(reason="one weight for each output feature, one to a partition"):
            nc.sync.dma_start(out=so_sb[:], in_=so.rearrange("(t p) o -> p (t o)", p=P))
        idx6 = load_list("idx6", offs6)
        idx7 = load_list("idx7", offs7)

        pages = [sb("page%d" % n, [P, G], F32) for n in range(2)]
        for page in pages:
            nc.vector.memset(page[:], 0.0)

        JH = J // 2
        JQ = J // 4
        xa = [sb("xa%d" % u, [P, 2, J], F32) for u in range(2)]
        xb = [sb("xb%d" % u, [P, 2, J], F32) for u in range(2)]
        xc = [sb("xc%d" % h, [P, JH, PACK], BF16) for h in range(2)]

        def add_pair(u, first, width):
            cols = slice(first, first + width)
            h, start = divmod(first, JH)
            nc.vector.tensor_tensor(
                out=xc[h][:, start : start + width, 2 * u : 2 * u + 2],
                in0=xa[u][:, :, cols].rearrange("p t j -> p j t"),
                in1=xb[u][:, :, cols].rearrange("p t j -> p j t"),
                op=ADD,
            )

        for t in range(PACK):
            if t < PACK - 1:
                fetch(xa[t // 2][:, t % 2, :], a_win[t], idx[:], ga_sb[:, t : t + 1])
            fetch(xb[t // 2][:, t % 2, :], b_win[t], idx2[:], gb_sb[:, t : t + 1])
            if t == PACK - 1:
                for first in range(0, J, JQ):
                    fetch(xa[1][:, 1, first : first + JQ], a_win[t],
                          idx[:, first // 16 : (first + JQ) // 16], ga_sb[:, t : t + 1])
            if t == 1:
                for h in range(2):
                    add_pair(0, h * JH, JH)
                xr_sc = sb("xr_sc", [P, O], U8)
                nc.vector.tensor_copy(out=xr_sc[:], in_=xr_plane[:].indirect(idx5[:]))
            if t == 2:
                w_codes = sb("w_codes", [P, PACK, P], I32)
                nc.vector.tensor_copy(
                    out=w_codes[:].rearrange("p t (c i) -> p c t i", i=4),
                    in_=w_raw[:].rearrange("p (c i t) -> p c t i", i=4, t=PACK),
                )
                w_plane = sb("w_plane", [P, PACK, P], U8)
                nc.vector.tensor_copy(out=w_plane[:], in_=w_plane_raw[:].rearrange("p (m t) -> p t m", t=PACK))

        xc_codes = [sb("xc_codes%d" % h, [P, JH], U32) for h in range(2)]
        xc_plane = [sb("xc_plane%d" % h, [P, JH], U8) for h in range(2)]
        for first in range(0, J, JQ):
            add_pair(1, first, JQ)
        for h in range(2):
            nc.vector.quantize_mx(out=xc_codes[h][:].bitcast(FP8X4), scales=xc_plane[h][:],
                                  in_=xc[h][:].rearrange("p j t -> p (j t)"))

        a0_acc = [psum.tile([P, JH], F32, name="a0_acc%d" % h) for h in range(2)]
        a_acc = [None] + [psum.tile([P, J], F32, name="a_acc%d" % t) for t in range(1, PACK)]

        def first_product(t, h):
            nc.tensor.matmul_mx(
                out=a0_acc[h][:] if t == 0 else a_acc[t][:, h * JH : (h + 1) * JH],
                lhsT=w_codes[:, t, :].bitcast(FP8X4), lhsT_scale=w_plane[:, t, :],
                rhs=xc_codes[h][:].bitcast(FP8X4), rhs_scale=xc_plane[h][:],
                start=True, stop=True,
            )

        first_product(0, 0)
        first_product(0, 1)
        for t in range(1, PACK):
            for h in range(2):
                first_product(t, h)

        OH = O // 2
        ha = []
        hl = [sb("hl%d" % u, [P, 2, O], F32) for u in range(2)]
        a_sb = [sb("a_sb%d" % t, [P, J], F32) for t in range(PACK)]

        def max_pair(u, h):
            cols = slice(h * OH, (h + 1) * OH)
            nc.vector.tensor_tensor(
                out=hid[h][:, :, 2 * u : 2 * u + 2],
                in0=ha[u][:, :, cols].rearrange("p t o -> p o t"),
                in1=hl[u][:, :, cols].rearrange("p t o -> p o t"),
                op=MAX,
            )

        def fetch_level(t):
            fetch(hl[t // 2][:, t % 2, :], l_win[t], idx4[:], sl_sb[:, t : t + 1])

        for t in range(PACK):
            fetch_level(t)
        for h in range(2):
            nc.vector.tensor_copy(out=a_sb[0][:, h * JH : (h + 1) * JH], in_=a0_acc[h][:])
        for t in range(1, PACK):
            nc.vector.tensor_copy(out=a_sb[t][:], in_=a_acc[t][:])
        xr_codes = sb("xr_codes", [P, O], U16)
        nc.vector.tensor_copy(out=xr_codes[:], in_=xr_win[:].indirect(idx5[:]))
        hid = [sb("hid0", [P, OH, PACK], BF16, tag="xr_win"), sb("hid1", [P, OH, PACK], BF16)]
        ha.append(sb("ha0", [P, 2, O], F32, tag="tl3"))
        for t in range(2):
            fetch(ha[0][:, t, :], a_sb[t], idx3[:], sa_sb[:, t : t + 1])
        ha.append(sb("ha1", [P, 2, O], F32))
        fetch(ha[1][:, 0, :], a_sb[2], idx3[:], sa_sb[:, 2:3])
        for h in range(2):
            fetch(ha[1][:, 1, h * OH : (h + 1) * OH], a_sb[PACK - 1],
                  idx3[:, h * OH // 16 : (h + 1) * OH // 16], sa_sb[:, PACK - 1 : PACK])
        for u in range(2):
            for h in range(2):
                max_pair(u, h)
        hid_codes = [sb("hid_codes%d" % h, [P, OH], U32) for h in range(2)]
        hid_plane = [sb("hid_plane%d" % h, [P, OH], U8) for h in range(2)]
        for h in range(2):
            nc.vector.quantize_mx(out=hid_codes[h][:].bitcast(FP8X4), scales=hid_plane[h][:],
                                  in_=hid[h][:].rearrange("p o t -> p (o t)"))

        p0_acc = [psum.tile([P, OH], F32, name="p0_acc%d" % h) for h in range(2)]
        p1_acc = psum.tile([P, O], F32, name="p1_acc")

        def reminder_product(acc, n, cols):
            nc.tensor.matmul_mx(
                out=acc,
                lhsT=ws_codes[:, n * P : (n + 1) * P].bitcast(FP8X4), lhsT_scale=ws_plane[:, n * P : (n + 1) * P],
                rhs=xr_codes[:, cols].bitcast(FP4X4), rhs_scale=xr_sc[:, cols],
                start=True, stop=False,
            )

        def output_product(acc, n, h, stop):
            nc.tensor.matmul_mx(
                out=acc,
                lhsT=wb_codes[:, 2 * n * P : 2 * (n + 1) * P].bitcast(FP4X4),
                lhsT_scale=wb_plane[:, n * P : (n + 1) * P],
                rhs=hid_codes[h][:].bitcast(FP8X4), rhs_scale=hid_plane[h][:],
                start=False, stop=stop,
            )

        for h in range(2):
            reminder_product(p0_acc[h][:], 0, slice(h * OH, (h + 1) * OH))
        reminder_product(p1_acc[:], 1, slice(0, O))
        for h in range(2):
            output_product(p0_acc[h][:], 0, h, True)
        for h in range(2):
            output_product(p1_acc[:, h * OH : (h + 1) * OH], 1, h, h == 1)

        p_sb = [sb("p_sb%d" % n, [P, O], F32) for n in range(2)]
        m0 = [sb("m0_%d" % n, [P, E], F32) for n in range(2)]
        nc.scalar.copy(out=p_sb[0][:, 0:OH], in_=p0_acc[0][:])
        nc.vector.tensor_copy(out=p_sb[0][:, OH:O], in_=p0_acc[1][:])
        nc.vector.tensor_copy(out=p_sb[1][:], in_=p1_acc[:])
        for n in range(2):
            fetch(m0[n][:], p_sb[n], idx6[:], so_sb[:, n : n + 1])
        for n in range(2):
            nc.vector.tensor_copy(out=pages[n][:].indirect(idx7[:]), in_=m0[n][:])
            nc.sync.dma_start(out=out[n * P : (n + 1) * P, :], in_=pages[n][:])
